import numpy as np
import ml_dtypes


def mxq(x, axis, fmt="e4m3"):
    dtype, down = {"e4m3": (ml_dtypes.float8_e4m3fn, 7), "e5m2": (ml_dtypes.float8_e5m2, 14)}[fmt]
    v = np.moveaxis(np.asarray(x, np.float32).astype(ml_dtypes.bfloat16).astype(np.float64), axis, -1)
    blocks = v.reshape(v.shape[:-1] + (-1, 32))
    amax = np.abs(blocks).max(-1, keepdims=True)
    byte = np.maximum(np.where(amax > 0, np.frexp(amax)[1] - 1 + 127, 0) - down, 1)
    scale = np.exp2(byte - 127.0)
    codes = (blocks / scale).astype(np.float32).astype(dtype).astype(np.float64)
    return np.moveaxis((codes * scale).reshape(v.shape), -1, axis)


WIDE = False


def mx_kscale(k):
    if not WIDE:
        return np.ones(k)
    levels = np.array([10, -10, 5, -5, 0])
    if k % 512:
        return np.exp2(np.random.permutation(np.resize(levels, k // 32))).repeat(32)
    a = np.empty((k // 512, 16))
    for p in range(k // 512):
        a[p, :8] = np.random.permutation(np.resize(levels, 8))
        for g in range(8):
            far = levels[np.abs(levels - a[p, g]) >= 10]
            a[p, g + 8] = far[np.random.randint(len(far))]
    return np.exp2(a.ravel()).repeat(32)


def f64(x):
    return np.asarray(x).astype(np.float64)


def striped(idx):
    return np.tile(idx.reshape(-1, 16).T, (8, 1)).astype(np.uint16)


def unstriped(offs):
    return offs[:16].T.reshape(-1).astype(np.int64)


def pack_weight(w):
    k, n = w.shape
    w = f64(np.asarray(w, np.float32).astype(ml_dtypes.bfloat16)).reshape(k // 32, 32, n)
    amax = np.abs(w).max(1)
    byte = np.clip(np.where(amax > 0, np.frexp(amax)[1] - 1 + 127 - 7, 1), 1, 254)
    scaled = (w * np.exp2(127.0 - byte)[:, None, :]).reshape(k, n).astype(np.float32)
    words = np.ascontiguousarray(scaled.reshape(k // 512, 128, 4, n).transpose(0, 1, 3, 2)).astype(ml_dtypes.float8_e4m3fn).view(np.uint8)
    return words, np.ascontiguousarray(byte.astype(np.uint8).reshape(k // 512, 16, n))


def unpack_weight(words, scales):
    g, p, n, _ = words.shape
    vals = np.ascontiguousarray(words).view(ml_dtypes.float8_e4m3fn).astype(np.float64) * np.repeat(np.exp2(scales.astype(np.float64) - 127.0), 8, axis=1)[..., None]
    return vals.transpose(0, 1, 3, 2).reshape(g * 512, n)


E2M1 = np.array([0.0, 0.5, 1.0, 1.5, 2.0, 3.0, 4.0, 6.0, -0.0, -0.5, -1.0, -1.5, -2.0, -3.0, -4.0, -6.0])


def pack_fp4(w):
    k, n = w.shape
    w = f64(np.asarray(w, np.float32).astype(ml_dtypes.bfloat16)).reshape(k // 32, 32, n)
    amax = np.abs(w).max(1)
    mant, ex = np.frexp(amax / 6.0)
    byte = np.clip(np.where(amax > 0, np.where(mant > 0.5, ex, ex - 1) + 127, 1), 1, 254)
    scaled = (w * np.exp2(127.0 - byte)[:, None, :]).reshape(k, n).astype(np.float32)
    c = np.ascontiguousarray(scaled.reshape(k // 512, 128, 4, n).transpose(0, 1, 3, 2)).astype(ml_dtypes.float4_e2m1fn).view(np.uint8) & 0xF
    words = (c[..., 0::2] | (c[..., 1::2] << 4)).reshape(k // 512, 128, 2 * n)
    return np.ascontiguousarray(words), np.ascontiguousarray(byte.astype(np.uint8).reshape(k // 512, 16, n))


def unpack_fp4(words, scales):
    g, _, n = scales.shape
    words = np.ascontiguousarray(words).reshape(g, 128, n, 2)
    nib = np.empty((g, 128, n, 4), np.uint8)
    nib[..., 0::2] = words & 0xF
    nib[..., 1::2] = words >> 4
    vals = E2M1[nib] * np.repeat(np.exp2(scales.astype(np.float64) - 127.0), 8, axis=1)[..., None]
    return vals.transpose(0, 1, 3, 2).reshape(g * 512, n)


def planes(y):
    n, m = y.shape
    v = y.astype(np.float32).astype(ml_dtypes.bfloat16).astype(np.float64).reshape(n // 32, 32, m)
    top = np.abs(v).max(1)
    byte = np.clip(np.where(top > 0, np.frexp(top)[1] - 1 + 127 - 7, 1), 1, 254)
    codes = (v * np.exp2(127.0 - byte)[:, None, :]).reshape(n, m).astype(np.float32).astype(ml_dtypes.float8_e4m3fn).view(np.uint8)
    words = codes.reshape(n // 512, 128, 4, m).transpose(0, 1, 3, 2)
    return np.ascontiguousarray(words), np.ascontiguousarray(byte.astype(np.uint8).reshape(n // 512, 16, m))


K, T, S, N, H, U = 512, 2048, 512, 512, 512, 1024


def setup_inputs():
    n = np.random.standard_normal
    s = mx_kscale(K)[:, None]
    u = mx_kscale(H)
    packed_xT = pack_weight(n((K, T)) * s)
    packed_w1 = pack_fp4(n((K, N)) / np.sqrt(K) / s)
    packed_w2 = pack_fp4(n((K, N)) / np.sqrt(K) / s)
    packed_w3 = pack_fp4(n((H, N)) / np.sqrt(H) / u[:, None])
    return {
        "x_words": packed_xT[0],
        "x_scales": packed_xT[1],
        "w1_words": packed_w1[0],
        "w1_scales": packed_w1[1],
        "w2_words": packed_w2[0],
        "w2_scales": packed_w2[1],
        "unit": (np.random.uniform(0.6, 1.4, (H, 1)) * u[:, None]).astype(np.float32),
        "w3_words": packed_w3[0],
        "w3_scales": packed_w3[1],
        "offs": striped(np.random.permutation(T)[:S]),
        "in_": striped(np.random.permutation(np.concatenate([np.arange(S), np.random.randint(0, S, U - S)]))),
        "ou": striped(np.random.permutation(np.concatenate([np.arange(S), np.random.randint(0, S, U - S)]))),
    }


def reference(x_words, x_scales, w1_words, w1_scales, w2_words, w2_scales, unit, w3_words, w3_scales, offs, in_, ou):
    xq = unpack_weight(x_words, x_scales)[:, unstriped(offs)]
    y = unpack_fp4(w1_words, w1_scales).T @ xq
    yi = y[:, unstriped(in_)]
    yo = y[:, unstriped(ou)]
    arg1 = yi + 0.6 * yo
    z1 = unpack_fp4(w2_words, w2_scales).T @ xq
    zo = z1[:, unstriped(ou)]
    hid = f64(unit) * (arg1 * arg1 - zo)
    out_0 = unpack_fp4(w3_words, w3_scales).T @ mxq(hid, 0, "e4m3")
    return (out_0,) + planes(out_0)

@@ -1,0 +1,203 @@
+from contextlib import ExitStack
+
+import concourse.mybir as mybir
+
+K, T, S, N, H, U = 512, 2048, 512, 512, 512, 1024
+FLOPS = 2 * K * S * H * 2 + 2 * H * N * U
+
+F32 = mybir.dt.float32
+BF16 = mybir.dt.bfloat16
+I32 = mybir.dt.int32
+U32 = mybir.dt.uint32
+U16 = mybir.dt.uint16
+U8 = mybir.dt.uint8
+FP8X4 = mybir.dt.float8_e4m3fn_x4
+FP4X4 = mybir.dt.float4_e2m1fn_x4
+MULT = mybir.AluOpType.mult
+ADD = mybir.AluOpType.add
+COPY = mybir.ActivationFunctionType.Copy
+
+P = 128
+PACK = 4
+CHUNK = 256
+LIST_ROWS = 16
+
+
+def load_scale_rows(queue, plane, scales):
+    for quad in range(4):
+        queue.dma_start(
+            out=plane[32 * quad : 32 * quad + 4, :].bitcast(I32),
+            in_=scales[0, 4 * quad : 4 * quad + 4, :].bitcast(I32),
+        )
+
+
+def deal_words(nc, dealt, raw):
+    nc.vector.tensor_copy(
+        out=dealt[:].rearrange("p (t m b) -> p t m b", t=PACK, b=2),
+        in_=raw[:].rearrange("p (m t b) -> p t m b", t=PACK, b=2),
+    )
+
+
+def deal_scales(nc, dealt, raw):
+    nc.vector.tensor_copy(
+        out=dealt[:].rearrange("p (t m) -> p t m", t=PACK),
+        in_=raw[:].rearrange("p (m t) -> p t m", t=PACK),
+    )
+
+
+def tile_picked_yorbres_sqr_po_kernel(
+    tc, x_words, x_scales, w1_words, w1_scales, w2_words, w2_scales, unit, w3_words, w3_scales,
+    offs, in_, ou, out_0, out_1, out_2,
+):
+    nc = tc.nc
+    chunks = U // CHUNK
+    cols16 = CHUNK // LIST_ROWS
+    with ExitStack() as ctx:
+        keep = ctx.enter_context(tc.tile_pool(name="keep", bufs=1))
+        psum = ctx.enter_context(tc.psum_pool(name="psum", bufs=8))
+
+        offs_sb = keep.tile([P, S // LIST_ROWS], U16, name="offs_sb")
+        in_sb = keep.tile([P, U // LIST_ROWS], U16, name="in_sb")
+        ou_sb = keep.tile([P, U // LIST_ROWS], U16, name="ou_sb")
+        x_codes = keep.tile([P, T], U32, name="x_codes", align_bytes=64)
+        x_plane = keep.tile([P, T], U8, name="x_plane", align_bytes=64)
+        raw_words = [keep.tile([P, 2 * N], U8, name=f"raw_words{i}", align_bytes=64) for i in range(3)]
+        raw_plane = [keep.tile([P, N], U8, name=f"raw_plane{i}", align_bytes=64) for i in range(3)]
+        w_words = [keep.tile([P, 2 * N], U8, name=f"w_words{i}", align_bytes=64) for i in range(2)]
+        w_plane = [keep.tile([P, N], U8, name=f"w_plane{i}", align_bytes=64) for i in range(2)]
+        unit_sb = keep.tile([P, PACK], F32, name="unit_sb")
+        neg_unit = keep.tile([P, PACK], F32, name="neg_unit")
+
+        nc.vector.memset(x_plane[:].bitcast(I32), 0)
+        nc.vector.memset(raw_plane[0][:].bitcast(I32), 0)
+        nc.gpsimd.memset(raw_plane[1][:].bitcast(I32), 0)
+        nc.gpsimd.memset(raw_plane[2][:].bitcast(I32), 0)
+
+        nc.sync.dma_start(offs_sb[:], offs)
+        load_scale_rows(nc.sync, x_plane, x_scales)
+        nc.sync.dma_start(out=raw_words[0][:].bitcast(I32), in_=w1_words[0].bitcast(I32))
+        nc.sync.dma_start(
+            out=x_codes[:].bitcast(I32), in_=x_words[0].rearrange("p n t -> p (n t)").bitcast(I32)
+        )
+        nc.sync.dma_start(ou_sb[:], ou)
+        load_scale_rows(nc.sync, raw_plane[0], w1_scales)
+        nc.sync.dma_start(in_sb[:], in_)
+        nc.sync.dma_start(out=unit_sb[:], in_=unit.rearrange("(p t) o -> p (t o)", t=PACK))
+        nc.sync.dma_start(out=raw_words[1][:].bitcast(I32), in_=w2_words[0].bitcast(I32))
+        nc.sync.dma_start(out=raw_words[2][:].bitcast(I32), in_=w3_words[0].bitcast(I32))
+        load_scale_rows(nc.scalar, raw_plane[1], w2_scales)
+        load_scale_rows(nc.sync, raw_plane[2], w3_scales)
+
+        picked_codes = keep.tile([P, S], U32, name="picked_codes", align_bytes=64)
+        picked_plane = keep.tile([P, S], U8, name="picked_plane", align_bytes=64)
+        nc.vector.tensor_copy(picked_plane[:], x_plane[:].indirect(offs_sb[:]))
+        deal_words(nc, w_words[0], raw_words[0])
+        nc.vector.tensor_copy(picked_codes[:], x_codes[:].indirect(offs_sb[:]))
+        deal_scales(nc, w_plane[0], raw_plane[0])
+        deal_words(nc, w_words[1], raw_words[1])
+        deal_scales(nc, w_plane[1], raw_plane[1])
+        nc.vector.tensor_scalar(neg_unit[:], unit_sb[:], -1.0, None, MULT)
+
+        def product(bank, w, t, codes, plane):
+            nc.tensor.matmul_mx(
+                out=bank,
+                lhsT=w_words[w][:, 2 * P * t : 2 * P * (t + 1)].bitcast(FP4X4),
+                lhsT_scale=w_plane[w][:, P * t : P * (t + 1)],
+                rhs=codes.bitcast(FP8X4),
+                rhs_scale=plane,
+                start=True,
+                stop=True,
+            )
+
+        y = [keep.tile([P, S], F32, name=f"y{t}") for t in range(PACK)]
+        z = [keep.tile([P, S], F32, name=f"z{t}") for t in range(PACK)]
+        for t in range(PACK):
+            bank = psum.tile([P, S], F32, name="bank")
+            product(bank[:], 0, t, picked_codes[:], picked_plane[:])
+            if t == 0:
+                nc.scalar.activation(y[t][:], bank[:], COPY)
+            else:
+                nc.vector.tensor_copy(y[t][:], bank[:])
+        for t in range(PACK):
+            bank = psum.tile([P, S], F32, name="bank")
+            product(bank[:], 1, t, picked_codes[:], picked_plane[:])
+            nc.scalar.activation(z[t][:], bank[:], COPY, scale=neg_unit[:, t : t + 1])
+
+        w_words.append(keep.tile([P, 2 * N], U8, name="w_words1", align_bytes=64))
+        w_plane.append(keep.tile([P, N], U8, name="w_plane1", align_bytes=64))
+        deal_words(nc, w_words[2], raw_words[2])
+        deal_scales(nc, w_plane[2], raw_plane[2])
+
+        out_plane = keep.tile([P, U], U8, name="out_plane", align_bytes=64)
+        out_rows = out_0.rearrange("(p t) r -> p t r", t=PACK)
+        out_words = out_1[0].rearrange("p r t -> p (r t)").bitcast(I32)
+        hid = {}
+        res = {}
+
+        def hidden(c):
+            entries = slice(c * cols16, (c + 1) * cols16)
+            hid[c] = keep.tile([P, PACK, CHUNK], F32, name=f"hid{c}")
+            outer = [keep.tile([P, CHUNK], F32, name=f"outer{c}_{t}") for t in range(PACK)]
+            arg = [keep.tile([P, CHUNK], F32, name=f"arg{c}_{t}") for t in range(PACK)]
+            square = [keep.tile([P, CHUNK], F32, name=f"square{c}_{t}") for t in range(PACK)]
+            for t in range(PACK):
+                nc.scalar.activation(outer[t][:], y[t][:].indirect(ou_sb[:, entries]), COPY, scale=0.6)
+            for pair in range(0, PACK, 2):
+                for t in (pair, pair + 1):
+                    nc.vector.tensor_tensor(arg[t][:], y[t][:].indirect(in_sb[:, entries]), outer[t][:], ADD)
+                for t in (pair, pair + 1):
+                    nc.vector.scalar_tensor_tensor(
+                        square[t][:], arg[t][:], unit_sb[:, t : t + 1], arg[t][:], MULT, MULT
+                    )
+                for t in (pair, pair + 1):
+                    nc.vector.tensor_tensor(hid[c][:, t, :], z[t][:].indirect(ou_sb[:, entries]), square[t][:], ADD)
+
+        def last_product(c):
+            grouped = keep.tile([P, CHUNK, PACK], BF16, name=f"hid_grouped{c}", align_bytes=64)
+            nc.scalar.copy(
+                grouped[:].rearrange("p (c i) t -> p c t i", i=4),
+                hid[c][:].rearrange("p t (c i) -> p c t i", i=4),
+            )
+            codes = keep.tile([P, CHUNK], U32, name=f"hid_codes{c}", align_bytes=64)
+            plane = keep.tile([P, CHUNK], U8, name=f"hid_plane{c}", align_bytes=64)
+            nc.vector.quantize_mx(
+                out=codes[:].bitcast(FP8X4), scales=plane[:], in_=grouped[:].rearrange("p c t -> p (c t)")
+            )
+            res[c] = keep.tile([P, PACK, CHUNK], F32, name=f"res{c}")
+            for pair in range(0, PACK, 2):
+                bank = psum.tile([P, 2 * CHUNK], F32, name="bank")
+                for t in (pair, pair + 1):
+                    product(bank[:, (t - pair) * CHUNK : (t - pair + 1) * CHUNK], 2, t, codes[:], plane[:])
+                nc.scalar.activation(
+                    res[c][:, pair : pair + 2, :].rearrange("p t r -> p (t r)"), bank[:], COPY
+                )
+            nc.sync.dma_start(out=out_rows[:, :, c * CHUNK : (c + 1) * CHUNK], in_=res[c][:])
+
+        def planes(c):
+            columns = slice(c * CHUNK, (c + 1) * CHUNK)
+            grouped = keep.tile([P, CHUNK, PACK], BF16, name=f"res_grouped{c}", align_bytes=64)
+            nc.vector.tensor_copy(
+                grouped[:].rearrange("p (c i) t -> p c t i", i=4),
+                res[c][:].rearrange("p t (c i) -> p c t i", i=4),
+            )
+            codes = keep.tile([P, CHUNK], U32, name=f"res_codes{c}", align_bytes=64)
+            nc.vector.quantize_mx(
+                out=codes[:].bitcast(FP8X4),
+                scales=out_plane[:, columns],
+                in_=grouped[:].rearrange("p c t -> p (c t)"),
+            )
+            nc.sync.dma_start(out=out_words[:, columns], in_=codes[:].bitcast(I32))
+
+        for step in range(chunks + 2):
+            if step < chunks:
+                hidden(step)
+            if 1 <= step <= chunks:
+                last_product(step - 1)
+            if step >= 2:
+                planes(step - 2)
+
+        for quad in range(4):
+            nc.sync.dma_start(
+                out=out_2[0, 4 * quad : 4 * quad + 4, :].bitcast(I32),
+                in_=out_plane[32 * quad : 32 * quad + 4, :].bitcast(I32),
+            )

@@ -1,6 +1,7 @@
 from contextlib import ExitStack
 
 import concourse.mybir as mybir
+from concourse.masks import make_identity
 
 K, T, S, N, H, U = 512, 2048, 512, 512, 512, 1024
 FLOPS = 2 * K * S * H * 2 + 2 * H * N * U
@@ -15,11 +16,14 @@ FP8X4 = mybir.dt.float8_e4m3fn_x4
 FP4X4 = mybir.dt.float4_e2m1fn_x4
 MULT = mybir.AluOpType.mult
 ADD = mybir.AluOpType.add
+SQUARE = mybir.ActivationFunctionType.Square
 COPY = mybir.ActivationFunctionType.Copy
 
 P = 128
 PACK = 4
-CHUNK = 256
+CHUNKS = [512,384,128]
+BANK = 512
+SPARE = 16
 LIST_ROWS = 16
 
 
@@ -38,8 +42,8 @@ def deal_words(nc, dealt, raw):
     )
 
 
-def deal_scales(nc, dealt, raw):
-    nc.vector.tensor_copy(
+def deal_scales(engine, dealt, raw):
+    engine.tensor_copy(
         out=dealt[:].rearrange("p (t m) -> p t m", t=PACK),
         in_=raw[:].rearrange("p (m t) -> p t m", t=PACK),
     )
@@ -50,11 +54,10 @@ def tile_picked_yorbres_sqr_po_kernel(
     offs, in_, ou, out_0, out_1, out_2,
 ):
     nc = tc.nc
-    chunks = U // CHUNK
-    cols16 = CHUNK // LIST_ROWS
     with ExitStack() as ctx:
         keep = ctx.enter_context(tc.tile_pool(name="keep", bufs=1))
-        psum = ctx.enter_context(tc.psum_pool(name="psum", bufs=8))
+        ring = ctx.enter_context(tc.tile_pool(name="ring", bufs=3))
+        psum = ctx.enter_context(tc.psum_pool(name="psum", bufs=1))
 
         offs_sb = keep.tile([P, S // LIST_ROWS], U16, name="offs_sb")
         in_sb = keep.tile([P, U // LIST_ROWS], U16, name="in_sb")
@@ -63,39 +66,43 @@ def tile_picked_yorbres_sqr_po_kernel(
         x_plane = keep.tile([P, T], U8, name="x_plane", align_bytes=64)
         raw_words = [keep.tile([P, 2 * N], U8, name=f"raw_words{i}", align_bytes=64) for i in range(3)]
         raw_plane = [keep.tile([P, N], U8, name=f"raw_plane{i}", align_bytes=64) for i in range(3)]
-        w_words = [keep.tile([P, 2 * N], U8, name=f"w_words{i}", align_bytes=64) for i in range(2)]
-        w_plane = [keep.tile([P, N], U8, name=f"w_plane{i}", align_bytes=64) for i in range(2)]
+        w_words = [keep.tile([P, 2 * N], U8, name=f"w_words{i}", align_bytes=64) for i in range(3)]
+        w_plane = [keep.tile([P, N], U8, name=f"w_plane{i}", align_bytes=64) for i in range(3)]
         unit_sb = keep.tile([P, PACK], F32, name="unit_sb")
         neg_unit = keep.tile([P, PACK], F32, name="neg_unit")
+        identity = keep.tile([P, P], F32, name="identity")
 
-        nc.vector.memset(x_plane[:].bitcast(I32), 0)
+        nc.gpsimd.memset(x_plane[:].bitcast(I32), 0)
         nc.vector.memset(raw_plane[0][:].bitcast(I32), 0)
-        nc.gpsimd.memset(raw_plane[1][:].bitcast(I32), 0)
+        nc.vector.memset(raw_plane[1][:].bitcast(I32), 0)
         nc.gpsimd.memset(raw_plane[2][:].bitcast(I32), 0)
+        make_identity(nc, identity[:])
 
+        for raw, words in ((raw_words[0], w1_words), (raw_words[1], w2_words)):
+            nc.sync.dma_start(out=raw[:].bitcast(I32), in_=words[0].bitcast(I32))
         nc.sync.dma_start(offs_sb[:], offs)
         load_scale_rows(nc.sync, x_plane, x_scales)
-        nc.sync.dma_start(out=raw_words[0][:].bitcast(I32), in_=w1_words[0].bitcast(I32))
         nc.sync.dma_start(
             out=x_codes[:].bitcast(I32), in_=x_words[0].rearrange("p n t -> p (n t)").bitcast(I32)
         )
-        nc.sync.dma_start(ou_sb[:], ou)
         load_scale_rows(nc.sync, raw_plane[0], w1_scales)
-        nc.sync.dma_start(in_sb[:], in_)
-        nc.sync.dma_start(out=unit_sb[:], in_=unit.rearrange("(p t) o -> p (t o)", t=PACK))
-        nc.sync.dma_start(out=raw_words[1][:].bitcast(I32), in_=w2_words[0].bitcast(I32))
         nc.sync.dma_start(out=raw_words[2][:].bitcast(I32), in_=w3_words[0].bitcast(I32))
-        load_scale_rows(nc.scalar, raw_plane[1], w2_scales)
+        nc.sync.dma_start(ou_sb[:], ou)
+        nc.sync.dma_start(in_sb[:], in_)
+        load_scale_rows(nc.sync, raw_plane[1], w2_scales)
+        nc.sync.dma_start(out=unit_sb[:], in_=unit.rearrange("(p t) o -> p (t o)", t=PACK))
         load_scale_rows(nc.sync, raw_plane[2], w3_scales)
 
         picked_codes = keep.tile([P, S], U32, name="picked_codes", align_bytes=64)
         picked_plane = keep.tile([P, S], U8, name="picked_plane", align_bytes=64)
-        nc.vector.tensor_copy(picked_plane[:], x_plane[:].indirect(offs_sb[:]))
         deal_words(nc, w_words[0], raw_words[0])
-        nc.vector.tensor_copy(picked_codes[:], x_codes[:].indirect(offs_sb[:]))
-        deal_scales(nc, w_plane[0], raw_plane[0])
         deal_words(nc, w_words[1], raw_words[1])
-        deal_scales(nc, w_plane[1], raw_plane[1])
+        nc.vector.tensor_copy(picked_plane[:], x_plane[:].indirect(offs_sb[:]))
+        deal_scales(nc.vector, w_plane[0], raw_plane[0])
+        deal_words(nc, w_words[2], raw_words[2])
+        nc.vector.tensor_copy(picked_codes[:], x_codes[:].indirect(offs_sb[:]))
+        deal_scales(nc.gpsimd, w_plane[1], raw_plane[1])
+        deal_scales(nc.gpsimd, w_plane[2], raw_plane[2])
         nc.vector.tensor_scalar(neg_unit[:], unit_sb[:], -1.0, None, MULT)
 
         def product(bank, w, t, codes, plane):
@@ -109,92 +116,141 @@ def tile_picked_yorbres_sqr_po_kernel(
                 stop=True,
             )
 
-        y = [keep.tile([P, S], F32, name=f"y{t}") for t in range(PACK)]
-        z = [keep.tile([P, S], F32, name=f"z{t}") for t in range(PACK)]
+        y = [keep.tile([P, S + SPARE], F32, name=f"y{t}") for t in range(PACK)]
+        z = [keep.tile([P, S + SPARE], F32, name=f"z{t}") for t in range(PACK)]
+        for window in y + z:
+            nc.gpsimd.memset(window[:, S:], 0.0)
         for t in range(PACK):
-            bank = psum.tile([P, S], F32, name="bank")
+            bank = psum.tile([P, BANK], F32, name="product_bank", bufs=4)
             product(bank[:], 0, t, picked_codes[:], picked_plane[:])
-            if t == 0:
-                nc.scalar.activation(y[t][:], bank[:], COPY)
+            if True:
+                nc.scalar.activation(y[t][:, 0:S], bank[:], COPY)
             else:
-                nc.vector.tensor_copy(y[t][:], bank[:])
-        for t in range(PACK):
-            bank = psum.tile([P, S], F32, name="bank")
-            product(bank[:], 1, t, picked_codes[:], picked_plane[:])
-            nc.scalar.activation(z[t][:], bank[:], COPY, scale=neg_unit[:, t : t + 1])
+                nc.vector.tensor_copy(y[t][:, 0:S], bank[:])
 
-        w_words.append(keep.tile([P, 2 * N], U8, name="w_words1", align_bytes=64))
-        w_plane.append(keep.tile([P, N], U8, name="w_plane1", align_bytes=64))
-        deal_words(nc, w_words[2], raw_words[2])
-        deal_scales(nc, w_plane[2], raw_plane[2])
+        def second_projection(t):
+            bank = psum.tile([P, BANK], F32, name="product_bank", bufs=4)
+            product(bank[:], 1, t, picked_codes[:], picked_plane[:])
+            if t%2==0:
+                nc.scalar.activation(z[t][:, 0:S], bank[:], COPY, scale=neg_unit[:, t : t + 1])
+            else:
+                nc.vector.tensor_scalar(z[t][:, 0:S], bank[:], neg_unit[:, t : t + 1], None, MULT)
+
 
         out_plane = keep.tile([P, U], U8, name="out_plane", align_bytes=64)
         out_rows = out_0.rearrange("(p t) r -> p t r", t=PACK)
         out_words = out_1[0].rearrange("p r t -> p (r t)").bitcast(I32)
-        hid = {}
-        res = {}
+        starts = [sum(CHUNKS[:c]) for c in range(len(CHUNKS))]
+        hid = [keep.tile([P, PACK, w], F32, name=f"hid{c}") for c, w in enumerate(CHUNKS)]
+        res = [keep.tile([P, PACK, w], F32, name=f"res{c}") for c, w in enumerate(CHUNKS)]
+        fetched = {}
+        fetched_z = {}
+        squares = {}
 
-        def hidden(c):
-            entries = slice(c * cols16, (c + 1) * cols16)
-            hid[c] = keep.tile([P, PACK, CHUNK], F32, name=f"hid{c}")
-            outer = [keep.tile([P, CHUNK], F32, name=f"outer{c}_{t}") for t in range(PACK)]
-            arg = [keep.tile([P, CHUNK], F32, name=f"arg{c}_{t}") for t in range(PACK)]
-            square = [keep.tile([P, CHUNK], F32, name=f"square{c}_{t}") for t in range(PACK)]
-            for t in range(PACK):
-                nc.scalar.activation(outer[t][:], y[t][:].indirect(ou_sb[:, entries]), COPY, scale=0.6)
-            for pair in range(0, PACK, 2):
-                for t in (pair, pair + 1):
-                    nc.vector.tensor_tensor(arg[t][:], y[t][:].indirect(in_sb[:, entries]), outer[t][:], ADD)
-                for t in (pair, pair + 1):
-                    nc.vector.scalar_tensor_tensor(
-                        square[t][:], arg[t][:], unit_sb[:, t : t + 1], arg[t][:], MULT, MULT
-                    )
-                for t in (pair, pair + 1):
-                    nc.vector.tensor_tensor(hid[c][:, t, :], z[t][:].indirect(ou_sb[:, entries]), square[t][:], ADD)
+        def fetch(c, t):
+            w = CHUNKS[c]
+            entries = slice(starts[c] // LIST_ROWS, (starts[c] + w) // LIST_ROWS)
+            y_inner = ring.tile([P, w], F32, name="y_inner")
+            y_outer = ring.tile([P, w], F32, name="y_outer")
+            nc.scalar.activation(y_outer[:], y[t][:].indirect(ou_sb[:, entries]), COPY, scale=0.6)
+            if False:
+                nc.scalar.activation(y_inner[:], y[t][:].indirect(in_sb[:, entries]), COPY)
+            else:
+                nc.vector.tensor_copy(y_inner[:], y[t][:].indirect(in_sb[:, entries]))
+            fetched[c, t] = (y_inner, y_outer)
+
+        def fetch_z(c, t):
+            w = CHUNKS[c]
+            entries = slice(starts[c] // LIST_ROWS, (starts[c] + w) // LIST_ROWS)
+            if c == 0:
+                second_projection(t)
+            z_outer = ring.tile([P, w], F32, name="z_outer", bufs=4)
+            if t>=2:
+                nc.scalar.activation(z_outer[:], z[t][:].indirect(ou_sb[:, entries]), COPY)
+            else:
+                nc.vector.tensor_copy(z_outer[:], z[t][:].indirect(ou_sb[:, entries]))
+            fetched_z[c, t] = z_outer
+
+        def square(c, t):
+            w = CHUNKS[c]
+            y_inner, y_outer = fetched[c, t]
+            bank = psum.tile([P, BANK], F32, name="sum_bank", bufs=2)
+            for b in range(0, w, P):
+                nc.tensor.matmul(bank[:, b : b + P], y_outer[:, b : b + P], identity[:], start=True, stop=False, is_transpose=True)
+                nc.tensor.matmul(bank[:, b : b + P], y_inner[:, b : b + P], identity[:], start=False, stop=True, is_transpose=True)
+            squares[c, t] = ring.tile([P, w], F32, name="squared")
+            nc.scalar.activation(squares[c, t][:], bank[:, 0:w], SQUARE)
+
+        def hidden(c, t):
+            w = CHUNKS[c]
+            bank = psum.tile([P, BANK], F32, name="back_bank", bufs=2)
+            for b in range(0, w, P):
+                nc.tensor.transpose(bank[:, b : b + P], squares[c, t][:, b : b + P], identity[:])
+            nc.vector.scalar_tensor_tensor(
+                hid[c][:, t, :], bank[:, 0:w], unit_sb[:, t : t + 1], fetched_z[c, t][:], MULT, ADD
+            )
+
+        def interleave(name, source, w, engine):
+            grouped = keep.tile([P, w, PACK], BF16, name=name, align_bytes=64)
+            copy = {"V": nc.vector.tensor_copy, "S": nc.scalar.copy, "G": nc.gpsimd.tensor_copy}[engine]
+            copy(
+                grouped[:].rearrange("p (c i) t -> p c t i", i=4),
+                source[:].rearrange("p t (c i) -> p c t i", i=4),
+            )
+            return grouped
+
+        grouped_hid = {}
+        grouped_res = {}
+
+        def round_hid(c):
+            grouped_hid[c] = interleave(f"hid_grouped{c}", hid[c], CHUNKS[c], 'V')
 
         def last_product(c):
-            grouped = keep.tile([P, CHUNK, PACK], BF16, name=f"hid_grouped{c}", align_bytes=64)
-            nc.scalar.copy(
-                grouped[:].rearrange("p (c i) t -> p c t i", i=4),
-                hid[c][:].rearrange("p t (c i) -> p c t i", i=4),
-            )
-            codes = keep.tile([P, CHUNK], U32, name=f"hid_codes{c}", align_bytes=64)
-            plane = keep.tile([P, CHUNK], U8, name=f"hid_plane{c}", align_bytes=64)
+            w = CHUNKS[c]
+            codes = keep.tile([P, w], U32, name=f"hid_codes{c}", align_bytes=64)
+            plane = keep.tile([P, w], U8, name=f"hid_plane{c}", align_bytes=64)
             nc.vector.quantize_mx(
-                out=codes[:].bitcast(FP8X4), scales=plane[:], in_=grouped[:].rearrange("p c t -> p (c t)")
+                out=codes[:].bitcast(FP8X4), scales=plane[:], in_=grouped_hid[c][:].rearrange("p c t -> p (c t)")
             )
-            res[c] = keep.tile([P, PACK, CHUNK], F32, name=f"res{c}")
-            for pair in range(0, PACK, 2):
-                bank = psum.tile([P, 2 * CHUNK], F32, name="bank")
-                for t in (pair, pair + 1):
-                    product(bank[:, (t - pair) * CHUNK : (t - pair + 1) * CHUNK], 2, t, codes[:], plane[:])
-                nc.scalar.activation(
-                    res[c][:, pair : pair + 2, :].rearrange("p t r -> p (t r)"), bank[:], COPY
-                )
-            nc.sync.dma_start(out=out_rows[:, :, c * CHUNK : (c + 1) * CHUNK], in_=res[c][:])
+            per_bank = BANK // w
+            for first in range(0, PACK, per_bank):
+                bank = psum.tile([P, BANK], F32, name="product_bank", bufs=4)
+                for j in range(per_bank):
+                    for n0, n1 in ([(0, 256), (256, 384)] if w == 384 else [(0, w)]):
+                        product(bank[:, j * w + n0 : j * w + n1], 2, first + j, codes[:, n0:n1], plane[:, n0:n1])
+                rows = res[c][:, first : first + per_bank, :].rearrange("p t r -> p (t r)")
+                if c<len(CHUNKS)-1 or first==0:
+                    nc.scalar.activation(rows, bank[:, 0 : per_bank * w], COPY)
+                else:
+                    nc.vector.tensor_copy(rows, bank[:, 0 : per_bank * w])
+            nc.sync.dma_start(out=out_rows[:, :, starts[c] : starts[c] + w], in_=res[c][:])
+
+        def round_res(c):
+            grouped_res[c] = interleave(f"res_grouped{c}", res[c], CHUNKS[c], 'V')
 
         def planes(c):
-            columns = slice(c * CHUNK, (c + 1) * CHUNK)
-            grouped = keep.tile([P, CHUNK, PACK], BF16, name=f"res_grouped{c}", align_bytes=64)
-            nc.vector.tensor_copy(
-                grouped[:].rearrange("p (c i) t -> p c t i", i=4),
-                res[c][:].rearrange("p t (c i) -> p c t i", i=4),
-            )
-            codes = keep.tile([P, CHUNK], U32, name=f"res_codes{c}", align_bytes=64)
+            w = CHUNKS[c]
+            columns = slice(starts[c], starts[c] + w)
+            codes = keep.tile([P, w], U32, name=f"res_codes{c}", align_bytes=64)
             nc.vector.quantize_mx(
                 out=codes[:].bitcast(FP8X4),
                 scales=out_plane[:, columns],
-                in_=grouped[:].rearrange("p c t -> p (c t)"),
+                in_=grouped_res[c][:].rearrange("p c t -> p (c t)"),
             )
             nc.sync.dma_start(out=out_words[:, columns], in_=codes[:].bitcast(I32))
 
-        for step in range(chunks + 2):
-            if step < chunks:
-                hidden(step)
-            if 1 <= step <= chunks:
-                last_product(step - 1)
-            if step >= 2:
-                planes(step - 2)
+        units = [(c, t) for c in range(len(CHUNKS)) for t in range(PACK)]
+        unit_stages = [fetch, fetch_z, square, hidden]
+        unit_lags = [0,2,1,3]
+        chunk_stages = [round_hid, last_product, round_res, planes]
+        chunk_lags = [4,5,8,9]
+        for step in range(len(units) + max(chunk_lags) + 1):
+            for lag, stage in zip(unit_lags, unit_stages):
+                if 0 <= step - lag < len(units):
+                    stage(*units[step - lag])
+            for lag, stage in zip(chunk_lags, chunk_stages):
+                if 0 <= step - lag < len(units) and units[step - lag][1] == PACK - 1:
+                    stage(units[step - lag][0])
 
         for quad in range(4):
             nc.sync.dma_start(

@@ -36,9 +36,9 @@ def load_scale_rows(queue, plane, scales):
 
 
 def deal_words(nc, dealt, raw):
-    nc.vector.tensor_copy(
-        out=dealt[:].rearrange("p (t m b) -> p t m b", t=PACK, b=2),
-        in_=raw[:].rearrange("p (m t b) -> p t m b", t=PACK, b=2),
+    nc.scalar.copy(
+        out=dealt[:].bitcast(U16).rearrange("p (t m) -> p t m", t=PACK),
+        in_=raw[:].bitcast(U16).rearrange("p (m t) -> p t m", t=PACK),
     )
 
 
@@ -78,8 +78,8 @@ def tile_picked_yorbres_sqr_po_kernel(
         nc.gpsimd.memset(raw_plane[2][:].bitcast(I32), 0)
         make_identity(nc, identity[:])
 
-        for raw, words in ((raw_words[0], w1_words), (raw_words[1], w2_words)):
-            nc.sync.dma_start(out=raw[:].bitcast(I32), in_=words[0].bitcast(I32))
+        nc.sync.dma_start(out=raw_words[0][:].bitcast(I32), in_=w1_words[0].bitcast(I32))
+        nc.sync.dma_start(out=raw_words[1][:].bitcast(I32), in_=w2_words[0].bitcast(I32))
         nc.sync.dma_start(offs_sb[:], offs)
         load_scale_rows(nc.sync, x_plane, x_scales)
         nc.sync.dma_start(
@@ -95,15 +95,14 @@ def tile_picked_yorbres_sqr_po_kernel(
 
         picked_codes = keep.tile([P, S], U32, name="picked_codes", align_bytes=64)
         picked_plane = keep.tile([P, S], U8, name="picked_plane", align_bytes=64)
-        deal_words(nc, w_words[0], raw_words[0])
-        deal_words(nc, w_words[1], raw_words[1])
+        for dealt, raw in zip(w_words, raw_words):
+            deal_words(nc, dealt, raw)
         nc.vector.tensor_copy(picked_plane[:], x_plane[:].indirect(offs_sb[:]))
         deal_scales(nc.vector, w_plane[0], raw_plane[0])
-        deal_words(nc, w_words[2], raw_words[2])
         nc.vector.tensor_copy(picked_codes[:], x_codes[:].indirect(offs_sb[:]))
-        deal_scales(nc.gpsimd, w_plane[1], raw_plane[1])
-        deal_scales(nc.gpsimd, w_plane[2], raw_plane[2])
+        deal_scales(nc.vector, w_plane[1], raw_plane[1])
         nc.vector.tensor_scalar(neg_unit[:], unit_sb[:], -1.0, None, MULT)
+        deal_scales(nc.vector, w_plane[2], raw_plane[2])
 
         def product(bank, w, t, codes, plane):
             nc.tensor.matmul_mx(

@@ -15,7 +15,7 @@ U8 = mybir.dt.uint8
 FP8X4 = mybir.dt.float8_e4m3fn_x4
 FP4X4 = mybir.dt.float4_e2m1fn_x4
 MULT = mybir.AluOpType.mult
-ADD = mybir.AluOpType.add
+SUBTRACT = mybir.AluOpType.subtract
 SQUARE = mybir.ActivationFunctionType.Square
 COPY = mybir.ActivationFunctionType.Copy
 
@@ -67,9 +67,8 @@ def tile_picked_yorbres_sqr_po_kernel(
         raw_words = [keep.tile([P, 2 * N], U8, name=f"raw_words{i}", align_bytes=64) for i in range(3)]
         raw_plane = [keep.tile([P, N], U8, name=f"raw_plane{i}", align_bytes=64) for i in range(3)]
         w_words = [keep.tile([P, 2 * N], U8, name=f"w_words{i}", align_bytes=64) for i in range(3)]
-        w_plane = [keep.tile([P, N], U8, name=f"w_plane{i}", align_bytes=64) for i in range(3)]
+        w_plane = [keep.tile([P, N], U8, name=f"w_plane{i}", align_bytes=64) for i in (1, 2)]
         unit_sb = keep.tile([P, PACK], F32, name="unit_sb")
-        neg_unit = keep.tile([P, PACK], F32, name="neg_unit")
         identity = keep.tile([P, P], F32, name="identity")
 
         nc.gpsimd.memset(x_plane[:].bitcast(I32), 0)
@@ -98,11 +97,11 @@ def tile_picked_yorbres_sqr_po_kernel(
         for dealt, raw in zip(w_words, raw_words):
             deal_words(nc, dealt, raw)
         nc.vector.tensor_copy(picked_plane[:], x_plane[:].indirect(offs_sb[:]))
-        deal_scales(nc.vector, w_plane[0], raw_plane[0])
         nc.vector.tensor_copy(picked_codes[:], x_codes[:].indirect(offs_sb[:]))
-        deal_scales(nc.vector, w_plane[1], raw_plane[1])
-        nc.vector.tensor_scalar(neg_unit[:], unit_sb[:], -1.0, None, MULT)
-        deal_scales(nc.vector, w_plane[2], raw_plane[2])
+        w_plane.insert(0, keep.tile([P, N], U8, name="x_codes", align_bytes=64))
+        deal_scales(nc.vector, w_plane[0], raw_plane[0])
+        deal_scales(nc.gpsimd, w_plane[1], raw_plane[1])
+        deal_scales(nc.gpsimd, w_plane[2], raw_plane[2])
 
         def product(bank, w, t, codes, plane):
             nc.tensor.matmul_mx(
@@ -131,9 +130,9 @@ def tile_picked_yorbres_sqr_po_kernel(
             bank = psum.tile([P, BANK], F32, name="product_bank", bufs=4)
             product(bank[:], 1, t, picked_codes[:], picked_plane[:])
             if t%2==0:
-                nc.scalar.activation(z[t][:, 0:S], bank[:], COPY, scale=neg_unit[:, t : t + 1])
+                nc.scalar.activation(z[t][:, 0:S], bank[:], COPY, scale=unit_sb[:, t : t + 1])
             else:
-                nc.vector.tensor_scalar(z[t][:, 0:S], bank[:], neg_unit[:, t : t + 1], None, MULT)
+                nc.vector.tensor_scalar(z[t][:, 0:S], bank[:], unit_sb[:, t : t + 1], None, MULT)
 
 
         out_plane = keep.tile([P, U], U8, name="out_plane", align_bytes=64)
@@ -186,15 +185,15 @@ def tile_picked_yorbres_sqr_po_kernel(
             for b in range(0, w, P):
                 nc.tensor.transpose(bank[:, b : b + P], squares[c, t][:, b : b + P], identity[:])
             nc.vector.scalar_tensor_tensor(
-                hid[c][:, t, :], bank[:, 0:w], unit_sb[:, t : t + 1], fetched_z[c, t][:], MULT, ADD
+                hid[c][:, t, :], bank[:, 0:w], unit_sb[:, t : t + 1], fetched_z[c, t][:], MULT, SUBTRACT
             )
 
         def interleave(name, source, w, engine):
             grouped = keep.tile([P, w, PACK], BF16, name=name, align_bytes=64)
             copy = {"V": nc.vector.tensor_copy, "S": nc.scalar.copy, "G": nc.gpsimd.tensor_copy}[engine]
             copy(
-                grouped[:].rearrange("p (c i) t -> p c t i", i=4),
-                source[:].rearrange("p t (c i) -> p c t i", i=4),
+                grouped[:].rearrange("p (c i) t -> p c t i", i=2),
+                source[:].rearrange("p t (c i) -> p c t i", i=2),
             )
             return grouped
 
@@ -222,7 +221,10 @@ def tile_picked_yorbres_sqr_po_kernel(
                     nc.scalar.activation(rows, bank[:, 0 : per_bank * w], COPY)
                 else:
                     nc.vector.tensor_copy(rows, bank[:, 0 : per_bank * w])
-            nc.sync.dma_start(out=out_rows[:, :, starts[c] : starts[c] + w], in_=res[c][:])
+                nc.sync.dma_start(
+                    out=out_rows[:, first : first + per_bank, starts[c] : starts[c] + w],
+                    in_=res[c][:, first : first + per_bank, :],
+                )
 
         def round_res(c):
             grouped_res[c] = interleave(f"res_grouped{c}", res[c], CHUNKS[c], 'V')

@@ -1,10 +1,9 @@
 from contextlib import ExitStack
 
 import concourse.mybir as mybir
-from concourse.masks import make_identity
 
 K, T, S, N, H, U = 512, 2048, 512, 512, 512, 1024
-FLOPS = 2 * K * S * H * 2 + 2 * H * N * U
+FLOPS = 2 * (2 * K * H * S) + 2 * H * N * U
 
 F32 = mybir.dt.float32
 BF16 = mybir.dt.bfloat16
@@ -15,23 +14,29 @@ U8 = mybir.dt.uint8
 FP8X4 = mybir.dt.float8_e4m3fn_x4
 FP4X4 = mybir.dt.float4_e2m1fn_x4
 MULT = mybir.AluOpType.mult
-SUBTRACT = mybir.AluOpType.subtract
-SQUARE = mybir.ActivationFunctionType.Square
+ADD = mybir.AluOpType.add
 COPY = mybir.ActivationFunctionType.Copy
+SQUARE = mybir.ActivationFunctionType.Square
 
 P = 128
 PACK = 4
-CHUNKS = [512,384,128]
-BANK = 512
-SPARE = 16
+QUADRANT = 32
+SCALE_ROWS = 4
 LIST_ROWS = 16
+BANK = 512
+BANKS = 8
+OUTER_WEIGHT = 0.6
+SPARE = 16
+CHUNKS = [512, 384, 128]
+PASS_WIDTHS = (512, 256, 128)
+RING = 3
 
 
-def load_scale_rows(queue, plane, scales):
-    for quad in range(4):
-        queue.dma_start(
-            out=plane[32 * quad : 32 * quad + 4, :].bitcast(I32),
-            in_=scales[0, 4 * quad : 4 * quad + 4, :].bitcast(I32),
+def load_plane(nc, plane, scales):
+    for quad in range(P // QUADRANT):
+        nc.sync.dma_start(
+            out=plane[QUADRANT * quad : QUADRANT * quad + SCALE_ROWS, :].bitcast(I32),
+            in_=scales[0, SCALE_ROWS * quad : SCALE_ROWS * (quad + 1), :].bitcast(I32),
         )
 
 
@@ -42,11 +47,21 @@ def deal_words(nc, dealt, raw):
     )
 
 
-def deal_scales(engine, dealt, raw):
+def deal_plane(engine, dealt, raw):
     engine.tensor_copy(
         out=dealt[:].rearrange("p (t m) -> p t m", t=PACK),
         in_=raw[:].rearrange("p (m t) -> p t m", t=PACK),
     )
+
+
+def passes(width):
+    ranges = []
+    start = 0
+    for step in PASS_WIDTHS:
+        if width - start >= step:
+            ranges.append((start, start + step))
+            start = start + step
+    return ranges
 
 
 def tile_picked_yorbres_sqr_po_kernel(
@@ -56,8 +71,8 @@ def tile_picked_yorbres_sqr_po_kernel(
     nc = tc.nc
     with ExitStack() as ctx:
         keep = ctx.enter_context(tc.tile_pool(name="keep", bufs=1))
-        ring = ctx.enter_context(tc.tile_pool(name="ring", bufs=3))
-        psum = ctx.enter_context(tc.psum_pool(name="psum", bufs=1))
+        ring = ctx.enter_context(tc.tile_pool(name="ring", bufs=RING))
+        psum = ctx.enter_context(tc.psum_pool(name="psum", bufs=BANKS))
 
         offs_sb = keep.tile([P, S // LIST_ROWS], U16, name="offs_sb")
         in_sb = keep.tile([P, U // LIST_ROWS], U16, name="in_sb")
@@ -67,30 +82,29 @@ def tile_picked_yorbres_sqr_po_kernel(
         raw_words = [keep.tile([P, 2 * N], U8, name=f"raw_words{i}", align_bytes=64) for i in range(3)]
         raw_plane = [keep.tile([P, N], U8, name=f"raw_plane{i}", align_bytes=64) for i in range(3)]
         w_words = [keep.tile([P, 2 * N], U8, name=f"w_words{i}", align_bytes=64) for i in range(3)]
-        w_plane = [keep.tile([P, N], U8, name=f"w_plane{i}", align_bytes=64) for i in (1, 2)]
+        w2_plane = keep.tile([P, N], U8, name="w2_plane", align_bytes=64)
         unit_sb = keep.tile([P, PACK], F32, name="unit_sb")
-        identity = keep.tile([P, P], F32, name="identity")
+        neg_unit = keep.tile([P, PACK], F32, name="neg_unit")
 
         nc.gpsimd.memset(x_plane[:].bitcast(I32), 0)
         nc.vector.memset(raw_plane[0][:].bitcast(I32), 0)
         nc.vector.memset(raw_plane[1][:].bitcast(I32), 0)
         nc.gpsimd.memset(raw_plane[2][:].bitcast(I32), 0)
-        make_identity(nc, identity[:])
 
         nc.sync.dma_start(out=raw_words[0][:].bitcast(I32), in_=w1_words[0].bitcast(I32))
         nc.sync.dma_start(out=raw_words[1][:].bitcast(I32), in_=w2_words[0].bitcast(I32))
         nc.sync.dma_start(offs_sb[:], offs)
-        load_scale_rows(nc.sync, x_plane, x_scales)
+        load_plane(nc, x_plane, x_scales)
         nc.sync.dma_start(
             out=x_codes[:].bitcast(I32), in_=x_words[0].rearrange("p n t -> p (n t)").bitcast(I32)
         )
-        load_scale_rows(nc.sync, raw_plane[0], w1_scales)
+        load_plane(nc, raw_plane[0], w1_scales)
         nc.sync.dma_start(out=raw_words[2][:].bitcast(I32), in_=w3_words[0].bitcast(I32))
         nc.sync.dma_start(ou_sb[:], ou)
         nc.sync.dma_start(in_sb[:], in_)
-        load_scale_rows(nc.sync, raw_plane[1], w2_scales)
+        load_plane(nc, raw_plane[1], w2_scales)
         nc.sync.dma_start(out=unit_sb[:], in_=unit.rearrange("(p t) o -> p (t o)", t=PACK))
-        load_scale_rows(nc.sync, raw_plane[2], w3_scales)
+        load_plane(nc, raw_plane[2], w3_scales)
 
         picked_codes = keep.tile([P, S], U32, name="picked_codes", align_bytes=64)
         picked_plane = keep.tile([P, S], U8, name="picked_plane", align_bytes=64)
@@ -98,16 +112,17 @@ def tile_picked_yorbres_sqr_po_kernel(
             deal_words(nc, dealt, raw)
         nc.vector.tensor_copy(picked_plane[:], x_plane[:].indirect(offs_sb[:]))
         nc.vector.tensor_copy(picked_codes[:], x_codes[:].indirect(offs_sb[:]))
-        w_plane.insert(0, keep.tile([P, N], U8, name="x_codes", align_bytes=64))
-        deal_scales(nc.vector, w_plane[0], raw_plane[0])
-        deal_scales(nc.gpsimd, w_plane[1], raw_plane[1])
-        deal_scales(nc.gpsimd, w_plane[2], raw_plane[2])
+        w1_plane = keep.tile([P, N], U8, name="w1_plane", tag="x_codes", align_bytes=64)
+        deal_plane(nc.vector, w1_plane, raw_plane[0])
+        deal_plane(nc.gpsimd, w2_plane, raw_plane[1])
+        nc.gpsimd.tensor_scalar(neg_unit[:], unit_sb[:], -1.0, 0.0, MULT, ADD)
+        w_plane = [w1_plane, w2_plane]
 
-        def product(bank, w, t, codes, plane):
+        def product(target, weight, t, codes, plane):
             nc.tensor.matmul_mx(
-                out=bank,
-                lhsT=w_words[w][:, 2 * P * t : 2 * P * (t + 1)].bitcast(FP4X4),
-                lhsT_scale=w_plane[w][:, P * t : P * (t + 1)],
+                out=target,
+                lhsT=w_words[weight][:, 2 * P * t : 2 * P * (t + 1)].bitcast(FP4X4),
+                lhsT_scale=w_plane[weight][:, P * t : P * (t + 1)],
                 rhs=codes.bitcast(FP8X4),
                 rhs_scale=plane,
                 start=True,
@@ -119,21 +134,23 @@ def tile_picked_yorbres_sqr_po_kernel(
         for window in y + z:
             nc.gpsimd.memset(window[:, S:], 0.0)
         for t in range(PACK):
-            bank = psum.tile([P, BANK], F32, name="product_bank", bufs=4)
+            bank = psum.tile([P, BANK], F32, name="bank")
             product(bank[:], 0, t, picked_codes[:], picked_plane[:])
-            if True:
+            if t < 2:
                 nc.scalar.activation(y[t][:, 0:S], bank[:], COPY)
             else:
                 nc.vector.tensor_copy(y[t][:, 0:S], bank[:])
 
         def second_projection(t):
-            bank = psum.tile([P, BANK], F32, name="product_bank", bufs=4)
+            bank = psum.tile([P, BANK], F32, name="bank")
             product(bank[:], 1, t, picked_codes[:], picked_plane[:])
-            if t%2==0:
-                nc.scalar.activation(z[t][:, 0:S], bank[:], COPY, scale=unit_sb[:, t : t + 1])
+            if t >= 2:
+                nc.scalar.activation(z[t][:, 0:S], bank[:], COPY, scale=neg_unit[:, t : t + 1])
             else:
-                nc.vector.tensor_scalar(z[t][:, 0:S], bank[:], unit_sb[:, t : t + 1], None, MULT)
-
+                nc.vector.tensor_scalar(z[t][:, 0:S], bank[:], neg_unit[:, t : t + 1], None, MULT)
+            if t == PACK - 1:
+                w_plane.append(keep.tile([P, N], U8, name="w3_plane", tag="w2_plane", align_bytes=64))
+                deal_plane(nc.vector, w_plane[2], raw_plane[2])
 
         out_plane = keep.tile([P, U], U8, name="out_plane", align_bytes=64)
         out_rows = out_0.rearrange("(p t) r -> p t r", t=PACK)
@@ -141,120 +158,111 @@ def tile_picked_yorbres_sqr_po_kernel(
         starts = [sum(CHUNKS[:c]) for c in range(len(CHUNKS))]
         hid = [keep.tile([P, PACK, w], F32, name=f"hid{c}") for c, w in enumerate(CHUNKS)]
         res = [keep.tile([P, PACK, w], F32, name=f"res{c}") for c, w in enumerate(CHUNKS)]
-        fetched = {}
-        fetched_z = {}
+        args = {}
+        z_outers = {}
         squares = {}
+        hid_rounded = {}
+        res_rounded = {}
 
-        def fetch(c, t):
-            w = CHUNKS[c]
-            entries = slice(starts[c] // LIST_ROWS, (starts[c] + w) // LIST_ROWS)
-            y_inner = ring.tile([P, w], F32, name="y_inner")
-            y_outer = ring.tile([P, w], F32, name="y_outer")
-            nc.scalar.activation(y_outer[:], y[t][:].indirect(ou_sb[:, entries]), COPY, scale=0.6)
-            if False:
-                nc.scalar.activation(y_inner[:], y[t][:].indirect(in_sb[:, entries]), COPY)
-            else:
-                nc.vector.tensor_copy(y_inner[:], y[t][:].indirect(in_sb[:, entries]))
-            fetched[c, t] = (y_inner, y_outer)
+        def entries(list_sb, c):
+            return list_sb[:, starts[c] // LIST_ROWS : (starts[c] + CHUNKS[c]) // LIST_ROWS]
+
+        def on_vector(c, t):
+            return c < len(CHUNKS) - 1 and t % 2 == 0
+
+        def fetch_arg(c, t):
+            args[c, t] = ring.tile([P, CHUNKS[c]], F32, name="arg")
+            y_outer = ring.tile([P, CHUNKS[c]], F32, name="y_outer")
+            nc.scalar.activation(y_outer[:], y[t][:].indirect(entries(ou_sb, c)), COPY, scale=OUTER_WEIGHT)
+            nc.vector.tensor_tensor(args[c, t][:], y[t][:].indirect(entries(in_sb, c)), y_outer[:], ADD)
 
         def fetch_z(c, t):
-            w = CHUNKS[c]
-            entries = slice(starts[c] // LIST_ROWS, (starts[c] + w) // LIST_ROWS)
             if c == 0:
                 second_projection(t)
-            z_outer = ring.tile([P, w], F32, name="z_outer", bufs=4)
-            if t>=2:
-                nc.scalar.activation(z_outer[:], z[t][:].indirect(ou_sb[:, entries]), COPY)
-            else:
-                nc.vector.tensor_copy(z_outer[:], z[t][:].indirect(ou_sb[:, entries]))
-            fetched_z[c, t] = z_outer
+            if not on_vector(c, t):
+                z_outers[c, t] = ring.tile([P, CHUNKS[c]], F32, name="z_outer")
+                nc.scalar.activation(z_outers[c, t][:], z[t][:].indirect(entries(ou_sb, c)), COPY)
 
         def square(c, t):
-            w = CHUNKS[c]
-            y_inner, y_outer = fetched[c, t]
-            bank = psum.tile([P, BANK], F32, name="sum_bank", bufs=2)
-            for b in range(0, w, P):
-                nc.tensor.matmul(bank[:, b : b + P], y_outer[:, b : b + P], identity[:], start=True, stop=False, is_transpose=True)
-                nc.tensor.matmul(bank[:, b : b + P], y_inner[:, b : b + P], identity[:], start=False, stop=True, is_transpose=True)
-            squares[c, t] = ring.tile([P, w], F32, name="squared")
-            nc.scalar.activation(squares[c, t][:], bank[:, 0:w], SQUARE)
+            squares[c, t] = ring.tile([P, CHUNKS[c]], F32, name="squared")
+            if on_vector(c, t):
+                nc.vector.scalar_tensor_tensor(
+                    squares[c, t][:], args[c, t][:], unit_sb[:, t : t + 1], args[c, t][:], MULT, MULT
+                )
+            else:
+                nc.scalar.activation(squares[c, t][:], args[c, t][:], SQUARE)
 
         def hidden(c, t):
-            w = CHUNKS[c]
-            bank = psum.tile([P, BANK], F32, name="back_bank", bufs=2)
-            for b in range(0, w, P):
-                nc.tensor.transpose(bank[:, b : b + P], squares[c, t][:, b : b + P], identity[:])
-            nc.vector.scalar_tensor_tensor(
-                hid[c][:, t, :], bank[:, 0:w], unit_sb[:, t : t + 1], fetched_z[c, t][:], MULT, SUBTRACT
-            )
+            if on_vector(c, t):
+                nc.vector.tensor_tensor(
+                    hid[c][:, t, :], z[t][:].indirect(entries(ou_sb, c)), squares[c, t][:], ADD
+                )
+            else:
+                nc.vector.scalar_tensor_tensor(
+                    hid[c][:, t, :], squares[c, t][:], unit_sb[:, t : t + 1], z_outers[c, t][:], MULT, ADD
+                )
 
-        def interleave(name, source, w, engine):
-            grouped = keep.tile([P, w, PACK], BF16, name=name, align_bytes=64)
-            copy = {"V": nc.vector.tensor_copy, "S": nc.scalar.copy, "G": nc.gpsimd.tensor_copy}[engine]
+        def round_and_group(name, source, width, copy):
+            grouped = keep.tile([P, width, PACK], BF16, name=name, align_bytes=64)
             copy(
                 grouped[:].rearrange("p (c i) t -> p c t i", i=2),
                 source[:].rearrange("p t (c i) -> p c t i", i=2),
             )
             return grouped
 
-        grouped_hid = {}
-        grouped_res = {}
-
         def round_hid(c):
-            grouped_hid[c] = interleave(f"hid_grouped{c}", hid[c], CHUNKS[c], 'V')
+            hid_rounded[c] = round_and_group(f"hid_rounded{c}", hid[c], CHUNKS[c], nc.vector.tensor_copy)
 
         def last_product(c):
-            w = CHUNKS[c]
-            codes = keep.tile([P, w], U32, name=f"hid_codes{c}", align_bytes=64)
-            plane = keep.tile([P, w], U8, name=f"hid_plane{c}", align_bytes=64)
+            width = CHUNKS[c]
+            codes = keep.tile([P, width], U32, name=f"hid_codes{c}", align_bytes=64)
+            plane = keep.tile([P, width], U8, name=f"hid_plane{c}", align_bytes=64)
             nc.vector.quantize_mx(
-                out=codes[:].bitcast(FP8X4), scales=plane[:], in_=grouped_hid[c][:].rearrange("p c t -> p (c t)")
+                out=codes[:].bitcast(FP8X4),
+                scales=plane[:],
+                in_=hid_rounded[c][:].rearrange("p c t -> p (c t)"),
             )
-            per_bank = BANK // w
+            per_bank = BANK // width
             for first in range(0, PACK, per_bank):
-                bank = psum.tile([P, BANK], F32, name="product_bank", bufs=4)
+                groups = slice(first, first + per_bank)
+                bank = psum.tile([P, BANK], F32, name="bank")
                 for j in range(per_bank):
-                    for n0, n1 in ([(0, 256), (256, 384)] if w == 384 else [(0, w)]):
-                        product(bank[:, j * w + n0 : j * w + n1], 2, first + j, codes[:, n0:n1], plane[:, n0:n1])
-                rows = res[c][:, first : first + per_bank, :].rearrange("p t r -> p (t r)")
-                if c<len(CHUNKS)-1 or first==0:
-                    nc.scalar.activation(rows, bank[:, 0 : per_bank * w], COPY)
-                else:
-                    nc.vector.tensor_copy(rows, bank[:, 0 : per_bank * w])
+                    for n0, n1 in passes(width):
+                        target = bank[:, j * width + n0 : j * width + n1]
+                        product(target, 2, first + j, codes[:, n0:n1], plane[:, n0:n1])
+                nc.scalar.activation(
+                    res[c][:, groups, :].rearrange("p t r -> p (t r)"), bank[:, 0 : per_bank * width], COPY
+                )
                 nc.sync.dma_start(
-                    out=out_rows[:, first : first + per_bank, starts[c] : starts[c] + w],
-                    in_=res[c][:, first : first + per_bank, :],
+                    out=out_rows[:, groups, starts[c] : starts[c] + width], in_=res[c][:, groups, :]
                 )
 
         def round_res(c):
-            grouped_res[c] = interleave(f"res_grouped{c}", res[c], CHUNKS[c], 'V')
+            res_rounded[c] = round_and_group(f"res_rounded{c}", res[c], CHUNKS[c], nc.vector.tensor_copy)
 
         def planes(c):
-            w = CHUNKS[c]
-            columns = slice(starts[c], starts[c] + w)
-            codes = keep.tile([P, w], U32, name=f"res_codes{c}", align_bytes=64)
+            columns = slice(starts[c], starts[c] + CHUNKS[c])
+            codes = keep.tile([P, CHUNKS[c]], U32, name=f"res_codes{c}", align_bytes=64)
             nc.vector.quantize_mx(
                 out=codes[:].bitcast(FP8X4),
                 scales=out_plane[:, columns],
-                in_=grouped_res[c][:].rearrange("p c t -> p (c t)"),
+                in_=res_rounded[c][:].rearrange("p c t -> p (c t)"),
             )
             nc.sync.dma_start(out=out_words[:, columns], in_=codes[:].bitcast(I32))
 
-        units = [(c, t) for c in range(len(CHUNKS)) for t in range(PACK)]
-        unit_stages = [fetch, fetch_z, square, hidden]
-        unit_lags = [0,2,1,3]
-        chunk_stages = [round_hid, last_product, round_res, planes]
-        chunk_lags = [4,5,8,9]
-        for step in range(len(units) + max(chunk_lags) + 1):
-            for lag, stage in zip(unit_lags, unit_stages):
-                if 0 <= step - lag < len(units):
-                    stage(*units[step - lag])
-            for lag, stage in zip(chunk_lags, chunk_stages):
-                if 0 <= step - lag < len(units) and units[step - lag][1] == PACK - 1:
-                    stage(units[step - lag][0])
+        items = [(c, t) for c in range(len(CHUNKS)) for t in range(PACK)]
+        item_stages = [(0, fetch_arg), (1, fetch_z), (1, square), (2, hidden)]
+        chunk_stages = [(4, round_hid), (5, last_product), (7, round_res), (8, planes)]
+        for step in range(len(items) + chunk_stages[-1][0]):
+            for lag, stage in item_stages:
+                if 0 <= step - lag < len(items):
+                    stage(*items[step - lag])
+            for lag, stage in chunk_stages:
+                if 0 <= step - lag < len(items) and items[step - lag][1] == PACK - 1:
+                    stage(items[step - lag][0])
 
-        for quad in range(4):
+        for quad in range(P // QUADRANT):
             nc.sync.dma_start(
-                out=out_2[0, 4 * quad : 4 * quad + 4, :].bitcast(I32),
-                in_=out_plane[32 * quad : 32 * quad + 4, :].bitcast(I32),
+                out=out_2[0, SCALE_ROWS * quad : SCALE_ROWS * (quad + 1), :].bitcast(I32),
+                in_=out_plane[QUADRANT * quad : QUADRANT * quad + SCALE_ROWS, :].bitcast(I32),
             )

from contextlib import ExitStack

import concourse.mybir as mybir

K, T, S, N, H, U = 512, 2048, 512, 512, 512, 1024
FLOPS = 2 * (2 * K * H * S) + 2 * H * N * U

F32 = mybir.dt.float32
BF16 = mybir.dt.bfloat16
I32 = mybir.dt.int32
U32 = mybir.dt.uint32
U16 = mybir.dt.uint16
U8 = mybir.dt.uint8
FP8X4 = mybir.dt.float8_e4m3fn_x4
FP4X4 = mybir.dt.float4_e2m1fn_x4
MULT = mybir.AluOpType.mult
ADD = mybir.AluOpType.add
COPY = mybir.ActivationFunctionType.Copy
SQUARE = mybir.ActivationFunctionType.Square

P = 128
PACK = 4
QUADRANT = 32
SCALE_ROWS = 4
LIST_ROWS = 16
BANK = 512
BANKS = 8
OUTER_WEIGHT = 0.6
SPARE = 16
CHUNKS = [512, 384, 128]
PASS_WIDTHS = (512, 256, 128)
RING = 3


def load_plane(nc, plane, scales):
    for quad in range(P // QUADRANT):
        nc.sync.dma_start(
            out=plane[QUADRANT * quad : QUADRANT * quad + SCALE_ROWS, :].bitcast(I32),
            in_=scales[0, SCALE_ROWS * quad : SCALE_ROWS * (quad + 1), :].bitcast(I32),
        )


def deal_words(nc, dealt, raw):
    nc.scalar.copy(
        out=dealt[:].bitcast(U16).rearrange("p (t m) -> p t m", t=PACK),
        in_=raw[:].bitcast(U16).rearrange("p (m t) -> p t m", t=PACK),
    )


def deal_plane(engine, dealt, raw):
    engine.tensor_copy(
        out=dealt[:].rearrange("p (t m) -> p t m", t=PACK),
        in_=raw[:].rearrange("p (m t) -> p t m", t=PACK),
    )


def passes(width):
    ranges = []
    start = 0
    for step in PASS_WIDTHS:
        if width - start >= step:
            ranges.append((start, start + step))
            start = start + step
    return ranges


def tile_picked_yorbres_sqr_po_kernel(
    tc, x_words, x_scales, w1_words, w1_scales, w2_words, w2_scales, unit, w3_words, w3_scales,
    offs, in_, ou, out_0, out_1, out_2,
):
    nc = tc.nc
    with ExitStack() as ctx:
        keep = ctx.enter_context(tc.tile_pool(name="keep", bufs=1))
        ring = ctx.enter_context(tc.tile_pool(name="ring", bufs=RING))
        psum = ctx.enter_context(tc.psum_pool(name="psum", bufs=BANKS))

        offs_sb = keep.tile([P, S // LIST_ROWS], U16, name="offs_sb")
        in_sb = keep.tile([P, U // LIST_ROWS], U16, name="in_sb")
        ou_sb = keep.tile([P, U // LIST_ROWS], U16, name="ou_sb")
        x_codes = keep.tile([P, T], U32, name="x_codes", align_bytes=64)
        x_plane = keep.tile([P, T], U8, name="x_plane", align_bytes=64)
        raw_words = [keep.tile([P, 2 * N], U8, name=f"raw_words{i}", align_bytes=64) for i in range(3)]
        raw_plane = [keep.tile([P, N], U8, name=f"raw_plane{i}", align_bytes=64) for i in range(3)]
        w_words = [keep.tile([P, 2 * N], U8, name=f"w_words{i}", align_bytes=64) for i in range(3)]
        w2_plane = keep.tile([P, N], U8, name="w2_plane", align_bytes=64)
        unit_sb = keep.tile([P, PACK], F32, name="unit_sb")
        neg_unit = keep.tile([P, PACK], F32, name="neg_unit")

        nc.gpsimd.memset(x_plane[:].bitcast(I32), 0)
        nc.vector.memset(raw_plane[0][:].bitcast(I32), 0)
        nc.vector.memset(raw_plane[1][:].bitcast(I32), 0)
        nc.gpsimd.memset(raw_plane[2][:].bitcast(I32), 0)

        nc.sync.dma_start(out=raw_words[0][:].bitcast(I32), in_=w1_words[0].bitcast(I32))
        nc.sync.dma_start(out=raw_words[1][:].bitcast(I32), in_=w2_words[0].bitcast(I32))
        nc.sync.dma_start(offs_sb[:], offs)
        load_plane(nc, x_plane, x_scales)
        nc.sync.dma_start(
            out=x_codes[:].bitcast(I32), in_=x_words[0].rearrange("p n t -> p (n t)").bitcast(I32)
        )
        load_plane(nc, raw_plane[0], w1_scales)
        nc.sync.dma_start(out=raw_words[2][:].bitcast(I32), in_=w3_words[0].bitcast(I32))
        nc.sync.dma_start(ou_sb[:], ou)
        nc.sync.dma_start(in_sb[:], in_)
        load_plane(nc, raw_plane[1], w2_scales)
        nc.sync.dma_start(out=unit_sb[:], in_=unit.rearrange("(p t) o -> p (t o)", t=PACK))
        load_plane(nc, raw_plane[2], w3_scales)

        picked_codes = keep.tile([P, S], U32, name="picked_codes", align_bytes=64)
        picked_plane = keep.tile([P, S], U8, name="picked_plane", align_bytes=64)
        for dealt, raw in zip(w_words, raw_words):
            deal_words(nc, dealt, raw)
        nc.vector.tensor_copy(picked_plane[:], x_plane[:].indirect(offs_sb[:]))
        nc.vector.tensor_copy(picked_codes[:], x_codes[:].indirect(offs_sb[:]))
        w1_plane = keep.tile([P, N], U8, name="w1_plane", tag="x_codes", align_bytes=64)
        deal_plane(nc.vector, w1_plane, raw_plane[0])
        deal_plane(nc.gpsimd, w2_plane, raw_plane[1])
        nc.gpsimd.tensor_scalar(neg_unit[:], unit_sb[:], -1.0, 0.0, MULT, ADD)
        w_plane = [w1_plane, w2_plane]

        def product(target, weight, t, codes, plane):
            nc.tensor.matmul_mx(
                out=target,
                lhsT=w_words[weight][:, 2 * P * t : 2 * P * (t + 1)].bitcast(FP4X4),
                lhsT_scale=w_plane[weight][:, P * t : P * (t + 1)],
                rhs=codes.bitcast(FP8X4),
                rhs_scale=plane,
                start=True,
                stop=True,
            )

        y = [keep.tile([P, S + SPARE], F32, name=f"y{t}") for t in range(PACK)]
        z = [keep.tile([P, S + SPARE], F32, name=f"z{t}") for t in range(PACK)]
        for window in y + z:
            nc.gpsimd.memset(window[:, S:], 0.0)
        for t in range(PACK):
            bank = psum.tile([P, BANK], F32, name="bank")
            product(bank[:], 0, t, picked_codes[:], picked_plane[:])
            if t < 2:
                nc.scalar.activation(y[t][:, 0:S], bank[:], COPY)
            else:
                nc.vector.tensor_copy(y[t][:, 0:S], bank[:])

        def second_projection(t):
            bank = psum.tile([P, BANK], F32, name="bank")
            product(bank[:], 1, t, picked_codes[:], picked_plane[:])
            if t >= 2:
                nc.scalar.activation(z[t][:, 0:S], bank[:], COPY, scale=neg_unit[:, t : t + 1])
            else:
                nc.vector.tensor_scalar(z[t][:, 0:S], bank[:], neg_unit[:, t : t + 1], None, MULT)
            if t == PACK - 1:
                w_plane.append(keep.tile([P, N], U8, name="w3_plane", tag="w2_plane", align_bytes=64))
                deal_plane(nc.vector, w_plane[2], raw_plane[2])

        out_plane = keep.tile([P, U], U8, name="out_plane", align_bytes=64)
        out_rows = out_0.rearrange("(p t) r -> p t r", t=PACK)
        out_words = out_1[0].rearrange("p r t -> p (r t)").bitcast(I32)
        starts = [sum(CHUNKS[:c]) for c in range(len(CHUNKS))]
        hid = [keep.tile([P, PACK, w], F32, name=f"hid{c}") for c, w in enumerate(CHUNKS)]
        res = [keep.tile([P, PACK, w], F32, name=f"res{c}") for c, w in enumerate(CHUNKS)]
        args = {}
        z_outers = {}
        squares = {}
        hid_rounded = {}
        res_rounded = {}

        def entries(list_sb, c):
            return list_sb[:, starts[c] // LIST_ROWS : (starts[c] + CHUNKS[c]) // LIST_ROWS]

        def on_vector(c, t):
            return c < len(CHUNKS) - 1 and t % 2 == 0

        def fetch_arg(c, t):
            args[c, t] = ring.tile([P, CHUNKS[c]], F32, name="arg")
            y_outer = ring.tile([P, CHUNKS[c]], F32, name="y_outer")
            nc.scalar.activation(y_outer[:], y[t][:].indirect(entries(ou_sb, c)), COPY, scale=OUTER_WEIGHT)
            nc.vector.tensor_tensor(args[c, t][:], y[t][:].indirect(entries(in_sb, c)), y_outer[:], ADD)

        def fetch_z(c, t):
            if c == 0:
                second_projection(t)
            if not on_vector(c, t):
                z_outers[c, t] = ring.tile([P, CHUNKS[c]], F32, name="z_outer")
                nc.scalar.activation(z_outers[c, t][:], z[t][:].indirect(entries(ou_sb, c)), COPY)

        def square(c, t):
            squares[c, t] = ring.tile([P, CHUNKS[c]], F32, name="squared")
            if on_vector(c, t):
                nc.vector.scalar_tensor_tensor(
                    squares[c, t][:], args[c, t][:], unit_sb[:, t : t + 1], args[c, t][:], MULT, MULT
                )
            else:
                nc.scalar.activation(squares[c, t][:], args[c, t][:], SQUARE)

        def hidden(c, t):
            if on_vector(c, t):
                nc.vector.tensor_tensor(
                    hid[c][:, t, :], z[t][:].indirect(entries(ou_sb, c)), squares[c, t][:], ADD
                )
            else:
                nc.vector.scalar_tensor_tensor(
                    hid[c][:, t, :], squares[c, t][:], unit_sb[:, t : t + 1], z_outers[c, t][:], MULT, ADD
                )

        def round_and_group(name, source, width, copy):
            grouped = keep.tile([P, width, PACK], BF16, name=name, align_bytes=64)
            copy(
                grouped[:].rearrange("p (c i) t -> p c t i", i=2),
                source[:].rearrange("p t (c i) -> p c t i", i=2),
            )
            return grouped

        def round_hid(c):
            hid_rounded[c] = round_and_group(f"hid_rounded{c}", hid[c], CHUNKS[c], nc.vector.tensor_copy)

        def last_product(c):
            width = CHUNKS[c]
            codes = keep.tile([P, width], U32, name=f"hid_codes{c}", align_bytes=64)
            plane = keep.tile([P, width], U8, name=f"hid_plane{c}", align_bytes=64)
            nc.vector.quantize_mx(
                out=codes[:].bitcast(FP8X4),
                scales=plane[:],
                in_=hid_rounded[c][:].rearrange("p c t -> p (c t)"),
            )
            per_bank = BANK // width
            for first in range(0, PACK, per_bank):
                groups = slice(first, first + per_bank)
                bank = psum.tile([P, BANK], F32, name="bank")
                for j in range(per_bank):
                    for n0, n1 in passes(width):
                        target = bank[:, j * width + n0 : j * width + n1]
                        product(target, 2, first + j, codes[:, n0:n1], plane[:, n0:n1])
                nc.scalar.activation(
                    res[c][:, groups, :].rearrange("p t r -> p (t r)"), bank[:, 0 : per_bank * width], COPY
                )
                nc.sync.dma_start(
                    out=out_rows[:, groups, starts[c] : starts[c] + width], in_=res[c][:, groups, :]
                )

        def round_res(c):
            res_rounded[c] = round_and_group(f"res_rounded{c}", res[c], CHUNKS[c], nc.vector.tensor_copy)

        def planes(c):
            columns = slice(starts[c], starts[c] + CHUNKS[c])
            codes = keep.tile([P, CHUNKS[c]], U32, name=f"res_codes{c}", align_bytes=64)
            nc.vector.quantize_mx(
                out=codes[:].bitcast(FP8X4),
                scales=out_plane[:, columns],
                in_=res_rounded[c][:].rearrange("p c t -> p (c t)"),
            )
            nc.sync.dma_start(out=out_words[:, columns], in_=codes[:].bitcast(I32))

        items = [(c, t) for c in range(len(CHUNKS)) for t in range(PACK)]
        item_stages = [(0, fetch_arg), (1, fetch_z), (1, square), (2, hidden)]
        chunk_stages = [(4, round_hid), (5, last_product), (7, round_res), (8, planes)]
        for step in range(len(items) + chunk_stages[-1][0]):
            for lag, stage in item_stages:
                if 0 <= step - lag < len(items):
                    stage(*items[step - lag])
            for lag, stage in chunk_stages:
                if 0 <= step - lag < len(items) and items[step - lag][1] == PACK - 1:
                    stage(items[step - lag][0])

        for quad in range(P // QUADRANT):
            nc.sync.dma_start(
                out=out_2[0, SCALE_ROWS * quad : SCALE_ROWS * (quad + 1), :].bitcast(I32),
                in_=out_plane[QUADRANT * quad : QUADRANT * quad + SCALE_ROWS, :].bitcast(I32),
            )
